import numpy as np
import ml_dtypes


def mxq(x, axis, fmt="e4m3"):
    dtype, down = {"e4m3": (ml_dtypes.float8_e4m3fn, 7), "e5m2": (ml_dtypes.float8_e5m2, 14)}[fmt]
    v = np.moveaxis(np.asarray(x, np.float32).astype(ml_dtypes.bfloat16).astype(np.float64), axis, -1)
    blocks = v.reshape(v.shape[:-1] + (-1, 32))
    amax = np.abs(blocks).max(-1, keepdims=True)
    byte = np.maximum(np.where(amax > 0, np.frexp(amax)[1] - 1 + 127, 0) - down, 1)
    scale = np.exp2(byte - 127.0)
    codes = (blocks / scale).astype(np.float32).astype(dtype).astype(np.float64)
    return np.moveaxis((codes * scale).reshape(v.shape), -1, axis)


WIDE = False


def mx_kscale(k):
    if not WIDE:
        return np.ones(k)
    levels = np.array([10, -10, 5, -5, 0])
    if k % 512:
        return np.exp2(np.random.permutation(np.resize(levels, k // 32))).repeat(32)
    a = np.empty((k // 512, 16))
    for p in range(k // 512):
        a[p, :8] = np.random.permutation(np.resize(levels, 8))
        for g in range(8):
            far = levels[np.abs(levels - a[p, g]) >= 10]
            a[p, g + 8] = far[np.random.randint(len(far))]
    return np.exp2(a.ravel()).repeat(32)


def f64(x):
    return np.asarray(x).astype(np.float64)


def split(x):
    m, e = np.frexp(f64(x))
    hi = np.ldexp(np.trunc(16.0 * m) / 16.0, e)
    return hi, f64(x) - hi


K, M, T = 512, 1536, 1024


def setup_inputs():
    n = np.random.standard_normal
    s = mx_kscale(K)[:, None]
    return {
        "w": (n((K, M)) / np.sqrt(K) / s).astype(np.float32),
        "x": (n((K, T)) * s).astype(np.float32),
        "g": (n((1536, 1024))).astype(np.float32),
    }


def reference(w, x, g):
    w_hi, w_lo = split(w)
    w_hi_, w_lo_ = mxq(w_hi, 0, "e4m3"), mxq(w_lo, 0, "e4m3")
    x_ = mxq(f64(x), 0, "e4m3")
    y = w_hi_.T @ x_ + w_lo_.T @ x_
    return f64(g) * y

from contextlib import ExitStack

import concourse.mybir as mybir

K, M, T = 512, 1536, 1024
FLOPS = 2 * 2 * K * M * T

F32 = mybir.dt.float32
BF16 = mybir.dt.bfloat16
I32 = mybir.dt.int32
U32 = mybir.dt.uint32
U8 = mybir.dt.uint8
FP8X4 = mybir.dt.float8_e4m3fn_x4
AND = mybir.AluOpType.bitwise_and

P = 128
J = 4
CHUNK = 512
CHUNKS = M // CHUNK
R = CHUNK // P
H = 512
HI_MASK = -1048576


def tile_mix_hilo_fm_mul_kernel(tc, w, x, g, out):
    nc = tc.nc
    with ExitStack() as ctx:
        pool = ctx.enter_context(tc.tile_pool(name="keep", bufs=1))
        psum = ctx.enter_context(tc.psum_pool(name="psum", bufs=1))
        ctx.enter_context(tc.manual_schedule())

        w_rows = w.rearrange("(p j) n -> p j n", j=J)
        g_rows = g.rearrange("(c p r) t -> c p r t", c=CHUNKS, r=R)
        out_rows = out.rearrange("(c p r) t -> c p r t", c=CHUNKS, r=R)

        w_first = pool.tile([P, J, CHUNK], F32, name="w_first", align_bytes=64)
        w_rest = pool.tile([P, J, M - CHUNK], F32, name="w_rest", align_bytes=64)
        x_raw = pool.tile([P, J, T], F32, name="x_raw", align_bytes=64)
        for j in (0, 2):
            nc.sync.dma_start(out=w_first[:, j : j + 2, :], in_=w_rows[:, j : j + 2, 0:CHUNK])
        nc.sync.dma_start(out=w_rest[:], in_=w_rows[:, :, CHUNK:M])
        nc.sync.dma_start(out=x_raw[:], in_=x.rearrange("(p j) t -> p j t", j=J))
        gate = []
        for c in range(CHUNKS):
            gate_c = pool.tile([P, R, T], F32, name="gate%d" % c, align_bytes=64)
            nc.sync.dma_start(out=gate_c[:], in_=g_rows[c])
            gate.append(gate_c)

        raw = [w_first[:], w_rest[:, :, 0:CHUNK], w_rest[:, :, CHUNK : 2 * CHUNK]]
        raw_bits = [
            w_first[:].bitcast(I32),
            w_rest[:].bitcast(I32)[:, :, 0:CHUNK],
            w_rest[:].bitcast(I32)[:, :, CHUNK : 2 * CHUNK],
        ]
        top, hi, lo, hi_codes, hi_scales, lo_codes, lo_scales, result = [], [], [], [], [], [], [], []
        for c in range(CHUNKS):
            top.append(pool.tile([P, J, CHUNK], F32, name="top%d" % c, align_bytes=64))
            hi.append(pool.tile([P, J * CHUNK], BF16, name="hi%d" % c, align_bytes=64))
            lo.append(pool.tile([P, J * CHUNK], BF16, name="lo%d" % c, align_bytes=64))
            hi_codes.append(pool.tile([P, CHUNK], U32, name="hi_codes%d" % c, align_bytes=64))
            hi_scales.append(pool.tile([P, CHUNK], U8, name="hi_scales%d" % c, align_bytes=64))
            lo_codes.append(pool.tile([P, CHUNK], U32, name="lo_codes%d" % c, align_bytes=64))
            lo_scales.append(pool.tile([P, CHUNK], U8, name="lo_scales%d" % c, align_bytes=64))
            result.append(pool.tile([P, R, T], F32, name="result%d" % c, align_bytes=64))
        x_bf, x_codes, x_scales = [], [], []
        for h in range(T // H):
            x_bf.append(pool.tile([P, J * H], BF16, name="x_bf%d" % h, align_bytes=64))
            x_codes.append(pool.tile([P, H], U32, name="x_codes%d" % h, align_bytes=64))
            x_scales.append(pool.tile([P, H], U8, name="x_scales%d" % h, align_bytes=64))

        def mask(c, j0, j1):
            nc.vector.tensor_scalar(
                out=top[c][:].bitcast(I32)[:, j0:j1, :],
                in0=raw_bits[c][:, j0:j1, :],
                scalar1=HI_MASK,
                scalar2=None,
                op0=AND,
            )

        def grouped(tile):
            return tile[:].rearrange("p (r q j) -> p q j r", r=R, j=J)

        def columns(ap):
            return ap.rearrange("p j (q r) -> p q j r", r=R)

        def take_hi(c):
            nc.scalar.copy(out=grouped(hi[c]), in_=columns(top[c][:]))

        def take_lo(c):
            nc.vector.tensor_sub(out=grouped(lo[c]), in0=columns(raw[c]), in1=columns(top[c][:]))

        def take_x(h):
            nc.scalar.copy(
                out=x_bf[h][:].rearrange("p (b i j) -> p b j i", i=4, j=J),
                in_=x_raw[:, :, h * H : (h + 1) * H].rearrange("p j (b i) -> p b j i", i=4),
            )

        def quantize(codes, scales, values):
            nc.vector.quantize_mx(out=codes[:].bitcast(FP8X4), scales=scales[:], in_=values[:])

        def quantize_hi(c):
            quantize(hi_codes[c], hi_scales[c], hi[c])

        def quantize_lo(c):
            quantize(lo_codes[c], lo_scales[c], lo[c])

        def quantize_x(h):
            quantize(x_codes[h], x_scales[h], x_bf[h])

        sums = {}

        def multiply(c, r, h):
            acc = psum.tile([P, H], F32, name="bank%d" % (R * h + r))
            cols = slice(r * P, (r + 1) * P)
            parts = ((hi_codes[c], hi_scales[c]), (lo_codes[c], lo_scales[c]))
            for i, (codes, scales) in enumerate(parts):
                nc.tensor.matmul_mx(
                    out=acc[:],
                    lhsT=codes[:, cols].bitcast(FP8X4),
                    lhsT_scale=scales[:, cols],
                    rhs=x_codes[h][:].bitcast(FP8X4),
                    rhs_scale=x_scales[h][:],
                    start=(i == 0),
                    stop=(i == 1),
                )
            sums[c, r, h] = acc

        def multiply_pair(c, r0):
            for r in (r0, r0 + 1):
                for h in range(T // H):
                    multiply(c, r, h)

        def finish_aside(c, r, h):
            cols = slice(h * H, (h + 1) * H)
            copied = pool.tile([P, H], F32, name="copied", bufs=3)
            nc.scalar.copy(out=copied[:], in_=sums[c, r, h][:])
            nc.gpsimd.tensor_tensor(
                out=result[c][:, r, cols], in0=copied[:], in1=gate[c][:, r, cols], op=mybir.AluOpType.mult
            )

        def finish(c, r, h):
            cols = slice(h * H, (h + 1) * H)
            nc.vector.tensor_mul(out=result[c][:, r, cols], in0=sums[c, r, h][:], in1=gate[c][:, r, cols])

        def finish_pair(c, r0):
            finish_aside(c, r0, 0)
            finish(c, r0 + 1, 0)
            finish(c, r0, 1)
            finish(c, r0 + 1, 1)
            nc.sync.dma_start(out=out_rows[c][:, r0 : r0 + 2, :], in_=result[c][:, r0 : r0 + 2, :])

        mask(0, 0, 2)
        mask(0, 2, 4)
        take_hi(0)
        take_lo(0)
        quantize_hi(0)
        mask(1, 0, 4)
        take_hi(1)
        quantize_lo(0)
        take_lo(1)
        mask(2, 0, 4)
        take_x(0)
        take_x(1)
        take_hi(2)
        quantize_x(0)
        for r in range(R):
            multiply(0, r, 0)
        quantize_hi(1)
        quantize_lo(1)
        take_lo(2)
        quantize_x(1)
        for r in range(R):
            multiply(0, r, 1)
        finish_pair(0, 0)
        multiply_pair(1, 0)
        quantize_hi(2)
        finish_pair(0, 2)
        multiply_pair(1, 2)
        quantize_lo(2)
        finish_pair(1, 0)
        multiply_pair(2, 0)
        finish_pair(1, 2)
        multiply_pair(2, 2)
        finish_pair(2, 0)
        finish_pair(2, 2)
